import numpy as np
import ml_dtypes


def mxq(x, axis, fmt="e4m3"):
    dtype, down = {"e4m3": (ml_dtypes.float8_e4m3fn, 7), "e5m2": (ml_dtypes.float8_e5m2, 14)}[fmt]
    v = np.moveaxis(np.asarray(x, np.float32).astype(ml_dtypes.bfloat16).astype(np.float64), axis, -1)
    blocks = v.reshape(v.shape[:-1] + (-1, 32))
    amax = np.abs(blocks).max(-1, keepdims=True)
    byte = np.maximum(np.where(amax > 0, np.frexp(amax)[1] - 1 + 127, 0) - down, 1)
    scale = np.exp2(byte - 127.0)
    codes = (blocks / scale).astype(np.float32).astype(dtype).astype(np.float64)
    return np.moveaxis((codes * scale).reshape(v.shape), -1, axis)


WIDE = False


def mx_kscale(k):
    if not WIDE:
        return np.ones(k)
    levels = np.array([10, -10, 5, -5, 0])
    if k % 512:
        return np.exp2(np.random.permutation(np.resize(levels, k // 32))).repeat(32)
    a = np.empty((k // 512, 16))
    for p in range(k // 512):
        a[p, :8] = np.random.permutation(np.resize(levels, 8))
        for g in range(8):
            far = levels[np.abs(levels - a[p, g]) >= 10]
            a[p, g + 8] = far[np.random.randint(len(far))]
    return np.exp2(a.ravel()).repeat(32)


def f64(x):
    return np.asarray(x).astype(np.float64)


def striped(idx):
    return np.tile(idx.reshape(-1, 16).T, (8, 1)).astype(np.uint16)


def unstriped(offs):
    return offs[:16].T.reshape(-1).astype(np.int64)


def striped8(idx):
    return np.concatenate([x.reshape(-1, 16).T for x in idx]).astype(np.uint16)


def runs(offs, k):
    lists = np.stack([offs[16 * r : 16 * r + 16].T.reshape(-1) for r in range(8)]).astype(np.int64)
    return lists[np.arange(k) % 512 // 64]


def pack_weight(w):
    k, n = w.shape
    w = f64(np.asarray(w, np.float32).astype(ml_dtypes.bfloat16)).reshape(k // 32, 32, n)
    amax = np.abs(w).max(1)
    byte = np.clip(np.where(amax > 0, np.frexp(amax)[1] - 1 + 127 - 7, 1), 1, 254)
    scaled = (w * np.exp2(127.0 - byte)[:, None, :]).reshape(k, n).astype(np.float32)
    words = np.ascontiguousarray(scaled.reshape(k // 512, 128, 4, n).transpose(0, 1, 3, 2)).astype(ml_dtypes.float8_e4m3fn).view(np.uint8)
    return words, np.ascontiguousarray(byte.astype(np.uint8).reshape(k // 512, 16, n))


def unpack_weight(words, scales):
    g, p, n, _ = words.shape
    vals = np.ascontiguousarray(words).view(ml_dtypes.float8_e4m3fn).astype(np.float64) * np.repeat(np.exp2(scales.astype(np.float64) - 127.0), 8, axis=1)[..., None]
    return vals.transpose(0, 1, 3, 2).reshape(g * 512, n)


def sigmoid(v):
    return 1.0 / (1.0 + np.exp(-np.maximum(v, -700.0)))


K, T, S, N, H = 512, 2048, 512, 512, 512


def setup_inputs():
    n = np.random.standard_normal
    s = mx_kscale(K)[:, None]
    u = mx_kscale(H)
    packed_xT = pack_weight(n((K, T)) * s)
    return {
        "x_words": packed_xT[0],
        "x_scales": packed_xT[1],
        "w1": (n((K, H)) / np.sqrt(K) / s).astype(np.float32),
        "gn": (np.random.uniform(0.5, 1.5, (H, 1)) * u[:, None]).astype(np.float32),
        "w2": (n((H, N)) / np.sqrt(H) / u[:, None]).astype(np.float32),
        "offs": striped(np.random.permutation(T)[:S]),
        "n1": striped8(np.stack([np.random.permutation(S) for _ in range(8)])),
        "n2": striped8(np.stack([np.random.permutation(S) for _ in range(8)])),
        "n3": striped8(np.stack([np.random.permutation(S) for _ in range(8)])),
        "n4": striped8(np.stack([np.random.permutation(S) for _ in range(8)])),
    }


def reference(x_words, x_scales, w1, gn, w2, offs, n1, n2, n3, n4):
    xq = unpack_weight(x_words, x_scales)[:, unstriped(offs)]
    y = mxq(f64(w1), 0, "e4m3").T @ xq
    z = f64(gn) * (y[np.arange(H)[:, None], runs(n1, H)] - (y[np.arange(H)[:, None], runs(n2, H)]))
    h = mxq(f64(w2), 0, "e4m3").T @ mxq(z, 0, "e4m3")
    return (h + h[np.arange(N)[:, None], runs(n3, N)]) * (sigmoid(y + y[np.arange(H)[:, None], runs(n4, H)]))

@@ -1,0 +1,155 @@
+from contextlib import ExitStack
+
+import concourse.mybir as mybir
+
+K, T, S, N, H = 512, 2048, 512, 512, 512
+FLOPS = 2 * K * H * S + 2 * H * N * S
+
+F32 = mybir.dt.float32
+BF16 = mybir.dt.bfloat16
+I32 = mybir.dt.int32
+U32 = mybir.dt.uint32
+U16 = mybir.dt.uint16
+U8 = mybir.dt.uint8
+FP8X4 = mybir.dt.float8_e4m3fn_x4
+ALU = mybir.AluOpType
+ACT = mybir.ActivationFunctionType
+
+P = 128
+PACK = 4
+WIN = 2 * S
+HALF = S // 2
+
+
+def deal_weight(engine_copy, grouped, raw, m0, m1):
+    dst = grouped[:].rearrange("p (t m j) -> p m t j", t=PACK, j=PACK)[:, m0:m1, :, :]
+    src = raw[:].rearrange("p j (m t) -> p m t j", t=PACK)[:, m0:m1, :, :]
+    engine_copy(dst, src)
+
+
+def tile_picked_skiptriebgap_none_p_kernel(
+    tc, x_words, x_scales, w1, gn, w2, offs, n1, n2, n3, n4, out
+):
+    nc = tc.nc
+    with ExitStack() as ctx:
+        lists = ctx.enter_context(tc.tile_pool(name="lists", bufs=1))
+        keep = ctx.enter_context(tc.tile_pool(name="keep", bufs=1))
+        psum = ctx.enter_context(tc.psum_pool(name="psum", bufs=1))
+
+        offs_t = lists.tile([P, S // 16], U16, name="offs_t")
+        n1_t = lists.tile([P, S // 16], U16, name="n1_t")
+        n2_t = lists.tile([P, S // 16], U16, name="n2_t")
+        n3_t = lists.tile([P, S // 16], U16, name="n3_t")
+        n4_t = lists.tile([P, S // 16], U16, name="n4_t")
+
+        xs = keep.tile([P, T], U8, name="xs", align_bytes=64)
+        xw = keep.tile([P, T], I32, name="xw", align_bytes=64)
+        w1_raw = keep.tile([P, PACK, H], F32, name="w1_raw")
+        w2_raw = keep.tile([P, PACK, N], F32, name="w2_raw")
+        gain = keep.tile([P, PACK], F32, name="gain")
+
+        nc.vector.memset(xs[:].bitcast(I32), 0)
+        nc.sync.dma_start(offs_t[:], offs)
+        nc.sync.dma_start(w1_raw[:], w1.rearrange("(p j) c -> p j c", j=PACK))
+        for q in range(4):
+            nc.scalar.dma_start(xs[:].bitcast(I32)[32 * q : 32 * q + 4, :], x_scales[0, 4 * q : 4 * q + 4, :].bitcast(I32))
+        nc.sync.dma_start(xw[:], x_words[0].rearrange("p n t -> p (n t)").bitcast(I32))
+        nc.sync.dma_start(gain[:], gn.rearrange("(p t) o -> p (t o)", t=PACK))
+        nc.sync.dma_start(n2_t[:], n2)
+        nc.sync.dma_start(n1_t[:], n1)
+        nc.sync.dma_start(w2_raw[:], w2.rearrange("(p j) c -> p j c", j=PACK))
+        nc.sync.dma_start(n4_t[:], n4)
+        nc.sync.dma_start(n3_t[:], n3)
+
+        warm = keep.tile([P, 2], F32, name="warm")
+        nc.gpsimd.memset(warm[:], 0.0)
+        nc.scalar.activation(warm[:, 1:2], warm[:, 0:1], ACT.Sigmoid)
+
+        g_win = [keep.tile([P, WIN], F32, name="g_win%d" % t) for t in range(PACK)]
+        y_win = [keep.tile([P, WIN], F32, name="y_win%d" % t) for t in range(PACK)]
+        for t in range(PACK):
+            nc.vector.memset(g_win[t][:, S:], 0.0)
+        for t in range(PACK):
+            nc.gpsimd.memset(y_win[t][:, S:], 0.0)
+
+        w1_b = keep.tile([P, PACK * H], BF16, name="w1_b", align_bytes=64)
+        w1_q = keep.tile([P, H], U32, name="w1_q", align_bytes=64)
+        w1_s = keep.tile([P, H], U8, name="w1_s", align_bytes=64)
+        xg = keep.tile([P, S], U32, name="xg", align_bytes=64)
+        sg = keep.tile([P, S], U8, name="sg", align_bytes=64)
+        deal_weight(nc.vector.tensor_copy, w1_b, w1_raw, 0, 64)
+        deal_weight(nc.scalar.copy, w1_b, w1_raw, 64, P)
+        nc.vector.tensor_copy(sg[:], xs[:].indirect(offs_t[:]))
+        nc.vector.quantize_mx(w1_q[:].bitcast(FP8X4), w1_s[:], w1_b[:])
+        nc.vector.tensor_copy(xg[:], xw[:].bitcast(U32).indirect(offs_t[:]))
+
+        y_ps = [psum.tile([P, S], F32, name="y_ps%d" % t) for t in range(PACK)]
+        for t in range(PACK):
+            cols = slice(P * t, P * (t + 1))
+            nc.tensor.matmul_mx(y_ps[t][:], lhsT=w1_q[:, cols].bitcast(FP8X4), lhsT_scale=w1_s[:, cols],
+                                rhs=xg[:].bitcast(FP8X4), rhs_scale=sg[:], start=True, stop=True)
+        for t in range(PACK):
+            nc.scalar.activation(g_win[t][:, :S], y_ps[t][:], ACT.Copy, scale=gain[:, t : t + 1])
+        y_cp = keep.tile([P, PACK, S], F32, name="y_cp")
+        for t in range(PACK):
+            nc.scalar.copy(y_win[t][:, :S], y_ps[t][:])
+            nc.scalar.copy(y_cp[:, t, :], y_ps[t][:])
+
+        w2_b = keep.tile([P, PACK * N], BF16, name="w2_b", align_bytes=64)
+        w2_q = keep.tile([P, N], U32, name="w2_q", align_bytes=64)
+        w2_s = keep.tile([P, N], U8, name="w2_s", align_bytes=64)
+        deal_weight(nc.scalar.copy, w2_b, w2_raw, 0, P)
+
+        sub = keep.tile([P, PACK, S], F32, name="sub")
+        z = keep.tile([P, PACK, S], F32, name="z")
+        for t in range(PACK):
+            nc.vector.tensor_copy(sub[:, t, :], g_win[t][:].indirect(n2_t[:]))
+            if t > 0:
+                nc.vector.tensor_tensor(z[:, t - 1, :], g_win[t - 1][:].indirect(n1_t[:]), sub[:, t - 1, :], ALU.subtract)
+        nc.vector.quantize_mx(w2_q[:].bitcast(FP8X4), w2_s[:], w2_b[:])
+        nc.vector.tensor_tensor(z[:, PACK - 1, :], g_win[PACK - 1][:].indirect(n1_t[:]), sub[:, PACK - 1, :], ALU.subtract)
+
+        z_b = keep.tile([P, PACK * S], BF16, name="z_b", tag="late", align_bytes=64)
+        z_q = keep.tile([P, S], U32, name="z_q", align_bytes=64)
+        z_s = keep.tile([P, S], U8, name="z_s", align_bytes=64)
+        for half in range(2):
+            c0, c1 = half * HALF // 4, (half + 1) * HALF // 4
+            nc.scalar.copy(z_b[:].rearrange("p (c i t) -> p c t i", i=4, t=PACK)[:, c0:c1, :, :],
+                           z[:].rearrange("p t (c i) -> p c t i", i=4)[:, c0:c1, :, :])
+
+        pre_early = keep.tile([P, 2, S], F32, name="pre_early")
+        gate = keep.tile([P, PACK, S], F32, name="gate")
+        for t in range(2):
+            nc.vector.tensor_tensor(pre_early[:, t, :], y_win[t][:].indirect(n4_t[:]), y_cp[:, t, :], ALU.add)
+
+        h_ps = [psum.tile([P, S], F32, name="h_ps%d" % t) for t in range(PACK)]
+        for half in range(2):
+            js = slice(half * HALF, (half + 1) * HALF)
+            nc.vector.quantize_mx(z_q[:, js].bitcast(FP8X4), z_s[:, js], z_b[:, PACK * half * HALF : PACK * (half + 1) * HALF])
+            for t in range(PACK):
+                cols = slice(P * t, P * (t + 1))
+                nc.tensor.matmul_mx(h_ps[t][:, js], lhsT=w2_q[:, cols].bitcast(FP8X4), lhsT_scale=w2_s[:, cols],
+                                    rhs=z_q[:, js].bitcast(FP8X4), rhs_scale=z_s[:, js], start=True, stop=True)
+
+        pre_late = keep.tile([P, 2, S], F32, name="pre_late", tag="late", align_bytes=64)
+        for t in range(2, PACK):
+            nc.vector.tensor_tensor(pre_late[:, t - 2, :], y_win[t][:].indirect(n4_t[:]), y_cp[:, t, :], ALU.add)
+
+        h_cp = keep.tile([P, PACK, S], F32, name="h_cp")
+        for t in range(2):
+            nc.scalar.activation(gate[:, t, :], pre_early[:, t, :], ACT.Sigmoid)
+        for t in range(PACK):
+            nc.scalar.copy(g_win[t][:, :S], h_ps[t][:])
+            nc.scalar.copy(h_cp[:, t, :], h_ps[t][:])
+        for t in range(2, PACK):
+            nc.scalar.activation(gate[:, t, :], pre_late[:, t - 2, :], ACT.Sigmoid)
+
+        hsum = keep.tile([P, PACK, S], F32, name="hsum")
+        res = keep.tile([P, PACK, S], F32, name="res")
+        out_rows = out.rearrange("(p t) j -> p t j", t=PACK)
+        for t in range(PACK + 1):
+            if t < PACK:
+                nc.vector.tensor_tensor(hsum[:, t, :], g_win[t][:].indirect(n3_t[:]), h_cp[:, t, :], ALU.add)
+            if t > 0:
+                nc.vector.tensor_tensor(res[:, t - 1, :], hsum[:, t - 1, :], gate[:, t - 1, :], ALU.mult)
+                nc.sync.dma_start(out_rows[:, t - 1, :], res[:, t - 1, :])

@@ -17,14 +17,21 @@ ACT = mybir.ActivationFunctionType
 
 P = 128
 PACK = 4
-WIN = 2 * S
+QUADRANT = 32
+GROUP = 16
+LINE = 4
+WINDOW = 2 * S
 HALF = S // 2
+WHOLE = slice(0, S)
+SPARE = slice(S, WINDOW)
+HALVES = (slice(0, HALF), slice(HALF, S))
+LIST_HALVES = (slice(0, HALF // GROUP), slice(HALF // GROUP, S // GROUP))
 
 
-def deal_weight(engine_copy, grouped, raw, m0, m1):
+def deal_weight(copy, grouped, raw, m0, m1):
     dst = grouped[:].rearrange("p (t m j) -> p m t j", t=PACK, j=PACK)[:, m0:m1, :, :]
     src = raw[:].rearrange("p j (m t) -> p m t j", t=PACK)[:, m0:m1, :, :]
-    engine_copy(dst, src)
+    copy(dst, src)
 
 
 def tile_picked_skiptriebgap_none_p_kernel(
@@ -36,120 +43,159 @@ def tile_picked_skiptriebgap_none_p_kernel(
         keep = ctx.enter_context(tc.tile_pool(name="keep", bufs=1))
         psum = ctx.enter_context(tc.psum_pool(name="psum", bufs=1))
 
-        offs_t = lists.tile([P, S // 16], U16, name="offs_t")
-        n1_t = lists.tile([P, S // 16], U16, name="n1_t")
-        n2_t = lists.tile([P, S // 16], U16, name="n2_t")
-        n3_t = lists.tile([P, S // 16], U16, name="n3_t")
-        n4_t = lists.tile([P, S // 16], U16, name="n4_t")
+        offs_t = lists.tile([P, S // GROUP], U16, name="offs_t")
+        n1_t = lists.tile([P, S // GROUP], U16, name="n1_t")
+        n2_t = lists.tile([P, S // GROUP], U16, name="n2_t")
+        n3_t = lists.tile([P, S // GROUP], U16, name="n3_t")
+        n4_t = lists.tile([P, S // GROUP], U16, name="n4_t")
 
         xs = keep.tile([P, T], U8, name="xs", align_bytes=64)
         xw = keep.tile([P, T], I32, name="xw", align_bytes=64)
         w1_raw = keep.tile([P, PACK, H], F32, name="w1_raw")
-        w2_raw = keep.tile([P, PACK, N], F32, name="w2_raw")
         gain = keep.tile([P, PACK], F32, name="gain")
-
-        nc.vector.memset(xs[:].bitcast(I32), 0)
+        nc.gpsimd.memset(xs[:].bitcast(I32), 0)
         nc.sync.dma_start(offs_t[:], offs)
         nc.sync.dma_start(w1_raw[:], w1.rearrange("(p j) c -> p j c", j=PACK))
-        for q in range(4):
-            nc.scalar.dma_start(xs[:].bitcast(I32)[32 * q : 32 * q + 4, :], x_scales[0, 4 * q : 4 * q + 4, :].bitcast(I32))
+        for q in range(P // QUADRANT):
+            nc.sync.dma_start(
+                xs[:].bitcast(I32)[QUADRANT * q : QUADRANT * q + 4, :], x_scales[0, 4 * q : 4 * q + 4, :].bitcast(I32)
+            )
         nc.sync.dma_start(xw[:], x_words[0].rearrange("p n t -> p (n t)").bitcast(I32))
         nc.sync.dma_start(gain[:], gn.rearrange("(p t) o -> p (t o)", t=PACK))
         nc.sync.dma_start(n2_t[:], n2)
         nc.sync.dma_start(n1_t[:], n1)
-        nc.sync.dma_start(w2_raw[:], w2.rearrange("(p j) c -> p j c", j=PACK))
         nc.sync.dma_start(n4_t[:], n4)
         nc.sync.dma_start(n3_t[:], n3)
 
-        warm = keep.tile([P, 2], F32, name="warm")
-        nc.gpsimd.memset(warm[:], 0.0)
-        nc.scalar.activation(warm[:, 1:2], warm[:, 0:1], ACT.Sigmoid)
-
-        g_win = [keep.tile([P, WIN], F32, name="g_win%d" % t) for t in range(PACK)]
-        y_win = [keep.tile([P, WIN], F32, name="y_win%d" % t) for t in range(PACK)]
+        scaled_win = [keep.tile([P, WINDOW], F32, name="scaled_win%d" % t) for t in range(PACK)]
+        y_win = [keep.tile([P, WINDOW], F32, name="y_win%d" % t) for t in range(PACK)]
         for t in range(PACK):
-            nc.vector.memset(g_win[t][:, S:], 0.0)
-        for t in range(PACK):
-            nc.gpsimd.memset(y_win[t][:, S:], 0.0)
+            nc.vector.memset(scaled_win[t][:, SPARE], 0.0)
 
         w1_b = keep.tile([P, PACK * H], BF16, name="w1_b", align_bytes=64)
-        w1_q = keep.tile([P, H], U32, name="w1_q", align_bytes=64)
+        w1_q = keep.tile([P, H], U32, name="w1_q", tag="w1q_then_z", align_bytes=64)
         w1_s = keep.tile([P, H], U8, name="w1_s", align_bytes=64)
         xg = keep.tile([P, S], U32, name="xg", align_bytes=64)
         sg = keep.tile([P, S], U8, name="sg", align_bytes=64)
-        deal_weight(nc.vector.tensor_copy, w1_b, w1_raw, 0, 64)
-        deal_weight(nc.scalar.copy, w1_b, w1_raw, 64, P)
+        deal_weight(nc.vector.tensor_copy, w1_b, w1_raw, 0, P // 2)
+        deal_weight(nc.scalar.copy, w1_b, w1_raw, P // 2, P)
         nc.vector.tensor_copy(sg[:], xs[:].indirect(offs_t[:]))
         nc.vector.quantize_mx(w1_q[:].bitcast(FP8X4), w1_s[:], w1_b[:])
-        nc.vector.tensor_copy(xg[:], xw[:].bitcast(U32).indirect(offs_t[:]))
+        for half in range(2):
+            nc.vector.tensor_copy(xg[:, HALVES[half]], xw[:].bitcast(U32).indirect(offs_t[:, LIST_HALVES[half]]))
 
-        y_ps = [psum.tile([P, S], F32, name="y_ps%d" % t) for t in range(PACK)]
-        for t in range(PACK):
+        w2_raw = keep.tile([P, PACK, N], F32, name="w2_raw", tag="w2_zb_pre", align_bytes=64)
+        nc.sync.dma_start(w2_raw[:], w2.rearrange("(p j) c -> p j c", j=PACK))
+
+        def product(acc, w_q, w_s, t, r_q, r_s, js):
             cols = slice(P * t, P * (t + 1))
-            nc.tensor.matmul_mx(y_ps[t][:], lhsT=w1_q[:, cols].bitcast(FP8X4), lhsT_scale=w1_s[:, cols],
-                                rhs=xg[:].bitcast(FP8X4), rhs_scale=sg[:], start=True, stop=True)
+            nc.tensor.matmul_mx(
+                acc,
+                lhsT=w_q[:, cols].bitcast(FP8X4),
+                lhsT_scale=w_s[:, cols],
+                rhs=r_q[:, js].bitcast(FP8X4),
+                rhs_scale=r_s[:, js],
+                start=True,
+                stop=True,
+            )
+
+        y0_ps = [psum.tile([P, HALF], F32, name="y0_ps%d" % half, tag="bank%d" % (PACK * half)) for half in range(2)]
+        y_parts = [[(y0_ps[half], HALVES[half]) for half in range(2)]] + [
+            [(psum.tile([P, S], F32, name="y_ps%d" % t, tag="bank%d" % t), WHOLE)] for t in range(1, PACK)
+        ]
         for t in range(PACK):
-            nc.scalar.activation(g_win[t][:, :S], y_ps[t][:], ACT.Copy, scale=gain[:, t : t + 1])
-        y_cp = keep.tile([P, PACK, S], F32, name="y_cp")
-        for t in range(PACK):
-            nc.scalar.copy(y_win[t][:, :S], y_ps[t][:])
-            nc.scalar.copy(y_cp[:, t, :], y_ps[t][:])
+            for acc, js in y_parts[t]:
+                product(acc[:], w1_q, w1_s, t, xg, sg, js)
+                nc.scalar.activation(scaled_win[t][:, js], acc[:], ACT.Copy, scale=gain[:, t : t + 1])
+
+        y_plain = [y_win[t ^ 1][:, SPARE] for t in range(PACK)]
+
+        def keep_y(t):
+            for acc, js in y_parts[t]:
+                nc.scalar.copy(y_win[t][:, js], acc[:])
+                nc.scalar.copy(y_plain[t][:, js], acc[:])
+
+        keep_y(0)
+        keep_y(1)
 
         w2_b = keep.tile([P, PACK * N], BF16, name="w2_b", align_bytes=64)
         w2_q = keep.tile([P, N], U32, name="w2_q", align_bytes=64)
         w2_s = keep.tile([P, N], U8, name="w2_s", align_bytes=64)
         deal_weight(nc.scalar.copy, w2_b, w2_raw, 0, P)
 
-        sub = keep.tile([P, PACK, S], F32, name="sub")
-        z = keep.tile([P, PACK, S], F32, name="z")
-        for t in range(PACK):
-            nc.vector.tensor_copy(sub[:, t, :], g_win[t][:].indirect(n2_t[:]))
-            if t > 0:
-                nc.vector.tensor_tensor(z[:, t - 1, :], g_win[t - 1][:].indirect(n1_t[:]), sub[:, t - 1, :], ALU.subtract)
-        nc.vector.quantize_mx(w2_q[:].bitcast(FP8X4), w2_s[:], w2_b[:])
-        nc.vector.tensor_tensor(z[:, PACK - 1, :], g_win[PACK - 1][:].indirect(n1_t[:]), sub[:, PACK - 1, :], ALU.subtract)
+        at_n2 = keep.tile([P, PACK, S], F32, name="at_n2")
+        z = keep.tile([P, PACK, S], F32, name="z", tag="w1q_then_z", align_bytes=64)
 
-        z_b = keep.tile([P, PACK * S], BF16, name="z_b", tag="late", align_bytes=64)
-        z_q = keep.tile([P, S], U32, name="z_q", align_bytes=64)
+        def subtract(t, js, entries):
+            nc.vector.tensor_tensor(z[:, t, js], scaled_win[t][:].indirect(entries), at_n2[:, t, js], ALU.subtract)
+
+        nc.vector.tensor_copy(at_n2[:, 0, :], scaled_win[0][:].indirect(n2_t[:]))
+        for t in range(1, PACK // 2 + 1):
+            nc.vector.tensor_copy(at_n2[:, t, :], scaled_win[t][:].indirect(n2_t[:]))
+            subtract(t - 1, WHOLE, n1_t[:])
+        nc.vector.tensor_copy(at_n2[:, PACK - 1, :], scaled_win[PACK - 1][:].indirect(n2_t[:]))
+
+        z_b = keep.tile([P, PACK * S], BF16, name="z_b", tag="w2_zb_pre", align_bytes=64)
+        z_q = keep.tile([P, S], U32, name="z_q", tag="zq_then_gate", align_bytes=64)
         z_s = keep.tile([P, S], U8, name="z_s", align_bytes=64)
         for half in range(2):
-            c0, c1 = half * HALF // 4, (half + 1) * HALF // 4
-            nc.scalar.copy(z_b[:].rearrange("p (c i t) -> p c t i", i=4, t=PACK)[:, c0:c1, :, :],
-                           z[:].rearrange("p t (c i) -> p c t i", i=4)[:, c0:c1, :, :])
+            for t in range(PACK // 2, PACK):
+                subtract(t, HALVES[half], n1_t[:, LIST_HALVES[half]])
+            lines = slice(half * HALF // LINE, (half + 1) * HALF // LINE)
+            nc.scalar.copy(
+                z_b[:].rearrange("p (c i t) -> p c t i", i=LINE, t=PACK)[:, lines, :, :],
+                z[:].rearrange("p t (c i) -> p c t i", i=LINE)[:, lines, :, :],
+            )
+        keep_y(2)
+        keep_y(3)
 
-        pre_early = keep.tile([P, 2, S], F32, name="pre_early")
-        gate = keep.tile([P, PACK, S], F32, name="gate")
-        for t in range(2):
-            nc.vector.tensor_tensor(pre_early[:, t, :], y_win[t][:].indirect(n4_t[:]), y_cp[:, t, :], ALU.add)
+        pre_early = keep.tile([P, S], F32, name="pre_early")
+        nc.vector.tensor_tensor(pre_early[:], y_win[0][:].indirect(n4_t[:]), y_plain[0], ALU.add)
+        nc.vector.quantize_mx(w2_q[:].bitcast(FP8X4), w2_s[:], w2_b[:])
+        nc.vector.quantize_mx(z_q[:].bitcast(FP8X4), z_s[:], z_b[:])
 
-        h_ps = [psum.tile([P, S], F32, name="h_ps%d" % t) for t in range(PACK)]
-        for half in range(2):
-            js = slice(half * HALF, (half + 1) * HALF)
-            nc.vector.quantize_mx(z_q[:, js].bitcast(FP8X4), z_s[:, js], z_b[:, PACK * half * HALF : PACK * (half + 1) * HALF])
-            for t in range(PACK):
-                cols = slice(P * t, P * (t + 1))
-                nc.tensor.matmul_mx(h_ps[t][:, js], lhsT=w2_q[:, cols].bitcast(FP8X4), lhsT_scale=w2_s[:, cols],
-                                    rhs=z_q[:, js].bitcast(FP8X4), rhs_scale=z_s[:, js], start=True, stop=True)
-
-        pre_late = keep.tile([P, 2, S], F32, name="pre_late", tag="late", align_bytes=64)
-        for t in range(2, PACK):
-            nc.vector.tensor_tensor(pre_late[:, t - 2, :], y_win[t][:].indirect(n4_t[:]), y_cp[:, t, :], ALU.add)
-
-        h_cp = keep.tile([P, PACK, S], F32, name="h_cp")
-        for t in range(2):
-            nc.scalar.activation(gate[:, t, :], pre_early[:, t, :], ACT.Sigmoid)
+        h_ps = [psum.tile([P, S], F32, name="h_ps%d" % t, tag="bank%d" % (2 * PACK - 1 - t)) for t in range(PACK)]
         for t in range(PACK):
-            nc.scalar.copy(g_win[t][:, :S], h_ps[t][:])
-            nc.scalar.copy(h_cp[:, t, :], h_ps[t][:])
-        for t in range(2, PACK):
-            nc.scalar.activation(gate[:, t, :], pre_late[:, t - 2, :], ACT.Sigmoid)
+            product(h_ps[t][:], w2_q, w2_s, t, z_q, z_s, WHOLE)
 
-        hsum = keep.tile([P, PACK, S], F32, name="hsum")
+        pre_late = keep.tile([P, PACK - 1, S], F32, name="pre_late", tag="w2_zb_pre", align_bytes=64)
+        for t in range(1, PACK):
+            nc.vector.tensor_tensor(pre_late[:, t - 1, :], y_win[t][:].indirect(n4_t[:]), y_plain[t], ALU.add)
+        pre = [pre_early[:]] + [pre_late[:, t - 1, :] for t in range(1, PACK)]
+
+        h_plain = keep.tile([P, PACK, S], F32, name="h_plain")
+        gate = keep.tile([P, PACK, S], F32, name="gate", tag="zq_then_gate", align_bytes=64)
+        h_sum = keep.tile([P, PACK, S], F32, name="h_sum")
         res = keep.tile([P, PACK, S], F32, name="res")
         out_rows = out.rearrange("(p t) j -> p t j", t=PACK)
-        for t in range(PACK + 1):
-            if t < PACK:
-                nc.vector.tensor_tensor(hsum[:, t, :], g_win[t][:].indirect(n3_t[:]), h_cp[:, t, :], ALU.add)
-            if t > 0:
-                nc.vector.tensor_tensor(res[:, t - 1, :], hsum[:, t - 1, :], gate[:, t - 1, :], ALU.mult)
-                nc.sync.dma_start(out_rows[:, t - 1, :], res[:, t - 1, :])
+
+        def keep_h(t):
+            nc.scalar.activation(scaled_win[t][:, WHOLE], h_ps[t][:], ACT.Copy, scale=0.5)
+            nc.scalar.activation(h_plain[:, t, :], h_ps[t][:], ACT.Copy, scale=0.5)
+
+        def add_h(t, js, entries):
+            nc.vector.tensor_tensor(h_sum[:, t, js], scaled_win[t][:].indirect(entries), h_plain[:, t, js], ALU.add)
+
+        def make_gate(t):
+            nc.scalar.activation(gate[:, t, :], pre[t], ACT.Tanh, scale=0.5)
+
+        def finish(t, js, queue):
+            nc.vector.scalar_tensor_tensor(res[:, t, js], gate[:, t, js], 1.0, h_sum[:, t, js], ALU.add, ALU.mult)
+            queue.dma_start(out_rows[:, t, js], res[:, t, js])
+
+        last = PACK - 1
+        keep_h(0)
+        add_h(0, WHOLE, n3_t[:])
+        for t in range(1, last):
+            keep_h(t)
+            add_h(t, WHOLE, n3_t[:])
+            make_gate(t - 1)
+            finish(t - 1, WHOLE, nc.sync)
+        make_gate(last - 1)
+        finish(last - 1, WHOLE, nc.sync)
+        keep_h(last)
+        for half in range(2):
+            add_h(last, HALVES[half], n3_t[:, LIST_HALVES[half]])
+        make_gate(last)
+        for half, queue in enumerate((nc.sync, nc.scalar)):
+            finish(last, HALVES[half], queue)

from contextlib import ExitStack

import concourse.mybir as mybir

K, T, S, N, H = 512, 2048, 512, 512, 512
FLOPS = 2 * K * H * S + 2 * H * N * S

F32 = mybir.dt.float32
BF16 = mybir.dt.bfloat16
I32 = mybir.dt.int32
U32 = mybir.dt.uint32
U16 = mybir.dt.uint16
U8 = mybir.dt.uint8
FP8X4 = mybir.dt.float8_e4m3fn_x4
ALU = mybir.AluOpType
ACT = mybir.ActivationFunctionType

P = 128
PACK = 4
QUADRANT = 32
GROUP = 16
LINE = 4
WINDOW = 2 * S
HALF = S // 2
WHOLE = slice(0, S)
SPARE = slice(S, WINDOW)
HALVES = (slice(0, HALF), slice(HALF, S))
LIST_HALVES = (slice(0, HALF // GROUP), slice(HALF // GROUP, S // GROUP))


def deal_weight(copy, grouped, raw, m0, m1):
    dst = grouped[:].rearrange("p (t m j) -> p m t j", t=PACK, j=PACK)[:, m0:m1, :, :]
    src = raw[:].rearrange("p j (m t) -> p m t j", t=PACK)[:, m0:m1, :, :]
    copy(dst, src)


def tile_picked_skiptriebgap_none_p_kernel(
    tc, x_words, x_scales, w1, gn, w2, offs, n1, n2, n3, n4, out
):
    nc = tc.nc
    with ExitStack() as ctx:
        lists = ctx.enter_context(tc.tile_pool(name="lists", bufs=1))
        keep = ctx.enter_context(tc.tile_pool(name="keep", bufs=1))
        psum = ctx.enter_context(tc.psum_pool(name="psum", bufs=1))

        offs_t = lists.tile([P, S // GROUP], U16, name="offs_t")
        n1_t = lists.tile([P, S // GROUP], U16, name="n1_t")
        n2_t = lists.tile([P, S // GROUP], U16, name="n2_t")
        n3_t = lists.tile([P, S // GROUP], U16, name="n3_t")
        n4_t = lists.tile([P, S // GROUP], U16, name="n4_t")

        xs = keep.tile([P, T], U8, name="xs", align_bytes=64)
        xw = keep.tile([P, T], I32, name="xw", align_bytes=64)
        w1_raw = keep.tile([P, PACK, H], F32, name="w1_raw")
        gain = keep.tile([P, PACK], F32, name="gain")
        nc.gpsimd.memset(xs[:].bitcast(I32), 0)
        nc.sync.dma_start(offs_t[:], offs)
        nc.sync.dma_start(w1_raw[:], w1.rearrange("(p j) c -> p j c", j=PACK))
        for q in range(P // QUADRANT):
            nc.sync.dma_start(
                xs[:].bitcast(I32)[QUADRANT * q : QUADRANT * q + 4, :], x_scales[0, 4 * q : 4 * q + 4, :].bitcast(I32)
            )
        nc.sync.dma_start(xw[:], x_words[0].rearrange("p n t -> p (n t)").bitcast(I32))
        nc.sync.dma_start(gain[:], gn.rearrange("(p t) o -> p (t o)", t=PACK))
        nc.sync.dma_start(n2_t[:], n2)
        nc.sync.dma_start(n1_t[:], n1)
        nc.sync.dma_start(n4_t[:], n4)
        nc.sync.dma_start(n3_t[:], n3)

        scaled_win = [keep.tile([P, WINDOW], F32, name="scaled_win%d" % t) for t in range(PACK)]
        y_win = [keep.tile([P, WINDOW], F32, name="y_win%d" % t) for t in range(PACK)]
        for t in range(PACK):
            nc.vector.memset(scaled_win[t][:, SPARE], 0.0)

        w1_b = keep.tile([P, PACK * H], BF16, name="w1_b", align_bytes=64)
        w1_q = keep.tile([P, H], U32, name="w1_q", tag="w1q_then_z", align_bytes=64)
        w1_s = keep.tile([P, H], U8, name="w1_s", align_bytes=64)
        xg = keep.tile([P, S], U32, name="xg", align_bytes=64)
        sg = keep.tile([P, S], U8, name="sg", align_bytes=64)
        deal_weight(nc.vector.tensor_copy, w1_b, w1_raw, 0, P // 2)
        deal_weight(nc.scalar.copy, w1_b, w1_raw, P // 2, P)
        nc.vector.tensor_copy(sg[:], xs[:].indirect(offs_t[:]))
        nc.vector.quantize_mx(w1_q[:].bitcast(FP8X4), w1_s[:], w1_b[:])
        for half in range(2):
            nc.vector.tensor_copy(xg[:, HALVES[half]], xw[:].bitcast(U32).indirect(offs_t[:, LIST_HALVES[half]]))

        w2_raw = keep.tile([P, PACK, N], F32, name="w2_raw", tag="w2_zb_pre", align_bytes=64)
        nc.sync.dma_start(w2_raw[:], w2.rearrange("(p j) c -> p j c", j=PACK))

        def product(acc, w_q, w_s, t, r_q, r_s, js):
            cols = slice(P * t, P * (t + 1))
            nc.tensor.matmul_mx(
                acc,
                lhsT=w_q[:, cols].bitcast(FP8X4),
                lhsT_scale=w_s[:, cols],
                rhs=r_q[:, js].bitcast(FP8X4),
                rhs_scale=r_s[:, js],
                start=True,
                stop=True,
            )

        y0_ps = [psum.tile([P, HALF], F32, name="y0_ps%d" % half, tag="bank%d" % (PACK * half)) for half in range(2)]
        y_parts = [[(y0_ps[half], HALVES[half]) for half in range(2)]] + [
            [(psum.tile([P, S], F32, name="y_ps%d" % t, tag="bank%d" % t), WHOLE)] for t in range(1, PACK)
        ]
        for t in range(PACK):
            for acc, js in y_parts[t]:
                product(acc[:], w1_q, w1_s, t, xg, sg, js)
                nc.scalar.activation(scaled_win[t][:, js], acc[:], ACT.Copy, scale=gain[:, t : t + 1])

        y_plain = [y_win[t ^ 1][:, SPARE] for t in range(PACK)]

        def keep_y(t):
            for acc, js in y_parts[t]:
                nc.scalar.copy(y_win[t][:, js], acc[:])
                nc.scalar.copy(y_plain[t][:, js], acc[:])

        keep_y(0)
        keep_y(1)

        w2_b = keep.tile([P, PACK * N], BF16, name="w2_b", align_bytes=64)
        w2_q = keep.tile([P, N], U32, name="w2_q", align_bytes=64)
        w2_s = keep.tile([P, N], U8, name="w2_s", align_bytes=64)
        deal_weight(nc.scalar.copy, w2_b, w2_raw, 0, P)

        at_n2 = keep.tile([P, PACK, S], F32, name="at_n2")
        z = keep.tile([P, PACK, S], F32, name="z", tag="w1q_then_z", align_bytes=64)

        def subtract(t, js, entries):
            nc.vector.tensor_tensor(z[:, t, js], scaled_win[t][:].indirect(entries), at_n2[:, t, js], ALU.subtract)

        nc.vector.tensor_copy(at_n2[:, 0, :], scaled_win[0][:].indirect(n2_t[:]))
        for t in range(1, PACK // 2 + 1):
            nc.vector.tensor_copy(at_n2[:, t, :], scaled_win[t][:].indirect(n2_t[:]))
            subtract(t - 1, WHOLE, n1_t[:])
        nc.vector.tensor_copy(at_n2[:, PACK - 1, :], scaled_win[PACK - 1][:].indirect(n2_t[:]))

        z_b = keep.tile([P, PACK * S], BF16, name="z_b", tag="w2_zb_pre", align_bytes=64)
        z_q = keep.tile([P, S], U32, name="z_q", tag="zq_then_gate", align_bytes=64)
        z_s = keep.tile([P, S], U8, name="z_s", align_bytes=64)
        for half in range(2):
            for t in range(PACK // 2, PACK):
                subtract(t, HALVES[half], n1_t[:, LIST_HALVES[half]])
            lines = slice(half * HALF // LINE, (half + 1) * HALF // LINE)
            nc.scalar.copy(
                z_b[:].rearrange("p (c i t) -> p c t i", i=LINE, t=PACK)[:, lines, :, :],
                z[:].rearrange("p t (c i) -> p c t i", i=LINE)[:, lines, :, :],
            )
        keep_y(2)
        keep_y(3)

        pre_early = keep.tile([P, S], F32, name="pre_early")
        nc.vector.tensor_tensor(pre_early[:], y_win[0][:].indirect(n4_t[:]), y_plain[0], ALU.add)
        nc.vector.quantize_mx(w2_q[:].bitcast(FP8X4), w2_s[:], w2_b[:])
        nc.vector.quantize_mx(z_q[:].bitcast(FP8X4), z_s[:], z_b[:])

        h_ps = [psum.tile([P, S], F32, name="h_ps%d" % t, tag="bank%d" % (2 * PACK - 1 - t)) for t in range(PACK)]
        for t in range(PACK):
            product(h_ps[t][:], w2_q, w2_s, t, z_q, z_s, WHOLE)

        pre_late = keep.tile([P, PACK - 1, S], F32, name="pre_late", tag="w2_zb_pre", align_bytes=64)
        for t in range(1, PACK):
            nc.vector.tensor_tensor(pre_late[:, t - 1, :], y_win[t][:].indirect(n4_t[:]), y_plain[t], ALU.add)
        pre = [pre_early[:]] + [pre_late[:, t - 1, :] for t in range(1, PACK)]

        h_plain = keep.tile([P, PACK, S], F32, name="h_plain")
        gate = keep.tile([P, PACK, S], F32, name="gate", tag="zq_then_gate", align_bytes=64)
        h_sum = keep.tile([P, PACK, S], F32, name="h_sum")
        res = keep.tile([P, PACK, S], F32, name="res")
        out_rows = out.rearrange("(p t) j -> p t j", t=PACK)

        def keep_h(t):
            nc.scalar.activation(scaled_win[t][:, WHOLE], h_ps[t][:], ACT.Copy, scale=0.5)
            nc.scalar.activation(h_plain[:, t, :], h_ps[t][:], ACT.Copy, scale=0.5)

        def add_h(t, js, entries):
            nc.vector.tensor_tensor(h_sum[:, t, js], scaled_win[t][:].indirect(entries), h_plain[:, t, js], ALU.add)

        def make_gate(t):
            nc.scalar.activation(gate[:, t, :], pre[t], ACT.Tanh, scale=0.5)

        def finish(t, js, queue):
            nc.vector.scalar_tensor_tensor(res[:, t, js], gate[:, t, js], 1.0, h_sum[:, t, js], ALU.add, ALU.mult)
            queue.dma_start(out_rows[:, t, js], res[:, t, js])

        last = PACK - 1
        keep_h(0)
        add_h(0, WHOLE, n3_t[:])
        for t in range(1, last):
            keep_h(t)
            add_h(t, WHOLE, n3_t[:])
            make_gate(t - 1)
            finish(t - 1, WHOLE, nc.sync)
        make_gate(last - 1)
        finish(last - 1, WHOLE, nc.sync)
        keep_h(last)
        for half in range(2):
            add_h(last, HALVES[half], n3_t[:, LIST_HALVES[half]])
        make_gate(last)
        for half, queue in enumerate((nc.sync, nc.scalar)):
            finish(last, HALVES[half], queue)
